import numpy as np
import ml_dtypes


def mxq(x, axis, fmt="e4m3"):
    dtype, down = {"e4m3": (ml_dtypes.float8_e4m3fn, 7), "e5m2": (ml_dtypes.float8_e5m2, 14)}[fmt]
    v = np.moveaxis(np.asarray(x, np.float32).astype(ml_dtypes.bfloat16).astype(np.float64), axis, -1)
    blocks = v.reshape(v.shape[:-1] + (-1, 32))
    amax = np.abs(blocks).max(-1, keepdims=True)
    byte = np.maximum(np.where(amax > 0, np.frexp(amax)[1] - 1 + 127, 0) - down, 1)
    scale = np.exp2(byte - 127.0)
    codes = (blocks / scale).astype(np.float32).astype(dtype).astype(np.float64)
    return np.moveaxis((codes * scale).reshape(v.shape), -1, axis)


WIDE = False


def mx_kscale(k, group=512):
    if not WIDE:
        return np.ones(k)
    levels = np.array([18, -18])
    if group != 512:
        return np.exp2(np.random.permutation(np.resize(levels, k // group))).repeat(group)
    if k % 512:
        return np.exp2(np.random.permutation(np.resize(levels, k // 32))).repeat(32)
    a = np.empty((k // 512, 16))
    for p in range(k // 512):
        a[p, :8] = np.random.permutation(np.resize(levels, 8))
        for g in range(8):
            far = levels[np.abs(levels - a[p, g]) >= 10]
            a[p, g + 8] = far[np.random.randint(len(far))]
    return np.exp2(a.ravel()).repeat(32)


def f64(x):
    return np.asarray(x).astype(np.float64)


G, D, M, N = 4, 128, 128, 512


def setup_inputs():
    n = np.random.standard_normal
    s_d = mx_kscale(D, 0)
    return {
        "x": (n((G, D, N)) * s_d[:, None]).astype(np.float32),
        "w": (n((D, M)) / np.sqrt(D) / s_d[:, None]).astype(np.float32),
        "b": (0.5 * n((M, 1)) + 1).astype(np.float32),
        "u": (n((G, M, N))).astype(np.float32),
    }


def reference(x, w, b, u):
    wq = mxq(f64(w), 0, "e4m3")
    xq = mxq(f64(x), 1, "e4m3")
    z = wq.T @ xq
    y = f64(u) * (z + f64(b))
    return y

@@ -1,0 +1,107 @@
+from contextlib import ExitStack
+
+import concourse.mybir as mybir
+
+G, D, M, N = 4, 128, 128, 512
+FLOPS = 2 * G * D * M * N
+
+F32 = mybir.dt.float32
+BF16 = mybir.dt.bfloat16
+U32 = mybir.dt.uint32
+U8 = mybir.dt.uint8
+FP8X4 = mybir.dt.float8_e4m3fn_x4
+ALU = mybir.AluOpType
+
+P = 128
+PACK = 4
+ROWS = D // PACK
+HALF = N // 2
+MM_N = 128
+VECTOR_COLS = 168
+
+
+def interleave(copy, grouped, raw, cols):
+    copy(
+        out=grouped[:, cols, :].rearrange("p (c i) j -> p c j i", i=4),
+        in_=raw[:, :, cols].rearrange("p j (c i) -> p c j i", i=4),
+    )
+
+
+def quantize(nc, codes, scales, grouped):
+    nc.vector.quantize_mx(
+        out=codes[:].bitcast(FP8X4),
+        scales=scales[:],
+        in_=grouped[:].rearrange("p c j -> p (c j)"),
+    )
+
+
+def tile_rows_mix_sgu_kernel(tc, x, w, b, u, out):
+    nc = tc.nc
+    x_rows = x.rearrange("g (p j) n -> (g p) j n", j=PACK)
+    w_rows = w.rearrange("(p j) m -> p j m", j=PACK)
+    u_rows = u.rearrange("g m n -> m g n")
+    out_rows = out.rearrange("g m n -> m g n")
+    halves = [slice(h * HALF, (h + 1) * HALF) for h in range(2)]
+
+    with ExitStack() as ctx:
+        sb = ctx.enter_context(tc.tile_pool(name="sb", bufs=1))
+        ps = ctx.enter_context(tc.psum_pool(name="ps", bufs=1))
+        ctx.enter_context(tc.manual_schedule())
+
+        x_raw = [sb.tile([P, PACK, HALF], F32, name=f"x_raw{h}", align_bytes=64) for h in range(2)]
+        x_grouped = [sb.tile([P, HALF, PACK], BF16, name=f"x_grouped{h}", align_bytes=64) for h in range(2)]
+        x_codes = [sb.tile([P, HALF], U32, name=f"x_codes{h}", align_bytes=64) for h in range(2)]
+        x_scales = [sb.tile([P, HALF], U8, name=f"x_scales{h}", align_bytes=64) for h in range(2)]
+        w_raw = sb.tile([P, PACK, M], F32, align_bytes=64)
+        w_grouped = sb.tile([P, M, PACK], BF16, align_bytes=64)
+        w_codes = sb.tile([P, M], U32, align_bytes=64)
+        w_scales = sb.tile([P, M], U8, align_bytes=64)
+        bias = sb.tile([P, 1], F32)
+        gate = [sb.tile([P, G, HALF], F32, name=f"gate{h}", align_bytes=64) for h in range(2)]
+        result = [[sb.tile([P, HALF], F32, name=f"result{h}_{g}", align_bytes=64) for g in range(G)] for h in range(2)]
+        z = [[ps.tile([P, HALF], F32, name=f"z{h}_{g}") for g in range(G)] for h in range(2)]
+
+        for g in range(G):
+            queue = nc.sync if g < 2 else nc.scalar
+            queue.dma_start(out=w_raw[ROWS * g : ROWS * (g + 1)], in_=w_rows)
+        nc.sync.dma_start(out=x_raw[0][:], in_=x_rows[:, :, halves[0]])
+        nc.scalar.dma_start(out=bias[:], in_=b)
+        nc.sync.dma_start(out=x_raw[1][:], in_=x_rows[:, :, halves[1]])
+        nc.sync.dma_start(out=gate[0][:, 0:2, :], in_=u_rows[:, 0:2, halves[0]])
+        nc.sync.dma_start(out=gate[0][:, 2:4, :], in_=u_rows[:, 2:4, halves[0]])
+        nc.sync.dma_start(out=gate[1][:], in_=u_rows[:, :, halves[1]])
+
+        def multiply(h):
+            for g in range(G):
+                rows = slice(ROWS * g, ROWS * (g + 1))
+                for c in range(0, HALF, MM_N):
+                    cols = slice(c, c + MM_N)
+                    nc.tensor.matmul_mx(
+                        out=z[h][g][:, cols],
+                        lhsT=w_codes[rows, :].bitcast(FP8X4),
+                        lhsT_scale=w_scales[rows, :],
+                        rhs=x_codes[h][rows, cols].bitcast(FP8X4),
+                        rhs_scale=x_scales[h][rows, cols],
+                        start=True,
+                        stop=True,
+                    )
+
+        interleave(nc.vector.tensor_copy, w_grouped, w_raw, slice(0, M))
+        quantize(nc, w_codes, w_scales, w_grouped)
+        for h in range(2):
+            interleave(nc.vector.tensor_copy, x_grouped[h], x_raw[h], slice(0, VECTOR_COLS))
+            interleave(nc.scalar.copy, x_grouped[h], x_raw[h], slice(VECTOR_COLS, HALF))
+            quantize(nc, x_codes[h], x_scales[h], x_grouped[h])
+            multiply(h)
+
+        for h in range(2):
+            for g in range(G):
+                nc.vector.scalar_tensor_tensor(
+                    out=result[h][g][:],
+                    in0=z[h][g][:],
+                    scalar=bias[:, 0:1],
+                    in1=gate[h][:, g, :],
+                    op0=ALU.add,
+                    op1=ALU.mult,
+                )
+                nc.sync.dma_start(out=out_rows[:, g, halves[h]], in_=result[h][g][:])

@@ -17,7 +17,7 @@ PACK = 4
 ROWS = D // PACK
 HALF = N // 2
 MM_N = 128
-VECTOR_COLS = 168
+VECTOR_COLS = (144, 96)
 
 
 def interleave(copy, grouped, raw, cols):
@@ -57,7 +57,7 @@ def tile_rows_mix_sgu_kernel(tc, x, w, b, u, out):
         w_codes = sb.tile([P, M], U32, align_bytes=64)
         w_scales = sb.tile([P, M], U8, align_bytes=64)
         bias = sb.tile([P, 1], F32)
-        gate = [sb.tile([P, G, HALF], F32, name=f"gate{h}", align_bytes=64) for h in range(2)]
+        gate = [[sb.tile([P, HALF], F32, name=f"gate{h}_{g}", align_bytes=64) for g in range(G)] for h in range(2)]
         result = [[sb.tile([P, HALF], F32, name=f"result{h}_{g}", align_bytes=64) for g in range(G)] for h in range(2)]
         z = [[ps.tile([P, HALF], F32, name=f"z{h}_{g}") for g in range(G)] for h in range(2)]
 
@@ -65,11 +65,11 @@ def tile_rows_mix_sgu_kernel(tc, x, w, b, u, out):
             queue = nc.sync if g < 2 else nc.scalar
             queue.dma_start(out=w_raw[ROWS * g : ROWS * (g + 1)], in_=w_rows)
         nc.sync.dma_start(out=x_raw[0][:], in_=x_rows[:, :, halves[0]])
-        nc.scalar.dma_start(out=bias[:], in_=b)
         nc.sync.dma_start(out=x_raw[1][:], in_=x_rows[:, :, halves[1]])
-        nc.sync.dma_start(out=gate[0][:, 0:2, :], in_=u_rows[:, 0:2, halves[0]])
-        nc.sync.dma_start(out=gate[0][:, 2:4, :], in_=u_rows[:, 2:4, halves[0]])
-        nc.sync.dma_start(out=gate[1][:], in_=u_rows[:, :, halves[1]])
+        nc.sync.dma_start(out=bias[:], in_=b)
+        for h in range(2):
+            for g in range(G):
+                nc.sync.dma_start(out=gate[h][g][:], in_=u_rows[:, g, halves[h]])
 
         def multiply(h):
             for g in range(G):
@@ -86,22 +86,32 @@ def tile_rows_mix_sgu_kernel(tc, x, w, b, u, out):
                         stop=True,
                     )
 
+        def group_x(h):
+            interleave(nc.vector.tensor_copy, x_grouped[h], x_raw[h], slice(0, VECTOR_COLS[h]))
+            interleave(nc.scalar.copy, x_grouped[h], x_raw[h], slice(VECTOR_COLS[h], HALF))
+
+        def finish(h, g):
+            nc.vector.scalar_tensor_tensor(
+                out=result[h][g][:],
+                in0=z[h][g][:],
+                scalar=bias[:, 0:1],
+                in1=gate[h][g][:],
+                op0=ALU.add,
+                op1=ALU.mult,
+            )
+            nc.sync.dma_start(out=out_rows[:, g, halves[h]], in_=result[h][g][:])
+
         interleave(nc.vector.tensor_copy, w_grouped, w_raw, slice(0, M))
         quantize(nc, w_codes, w_scales, w_grouped)
-        for h in range(2):
-            interleave(nc.vector.tensor_copy, x_grouped[h], x_raw[h], slice(0, VECTOR_COLS))
-            interleave(nc.scalar.copy, x_grouped[h], x_raw[h], slice(VECTOR_COLS, HALF))
-            quantize(nc, x_codes[h], x_scales[h], x_grouped[h])
-            multiply(h)
-
-        for h in range(2):
-            for g in range(G):
-                nc.vector.scalar_tensor_tensor(
-                    out=result[h][g][:],
-                    in0=z[h][g][:],
-                    scalar=bias[:, 0:1],
-                    in1=gate[h][:, g, :],
-                    op0=ALU.add,
-                    op1=ALU.mult,
-                )
-                nc.sync.dma_start(out=out_rows[:, g, halves[h]], in_=result[h][g][:])
+        group_x(0)
+        quantize(nc, x_codes[0], x_scales[0], x_grouped[0])
+        multiply(0)
+        group_x(1)
+        finish(0, 0)
+        finish(0, 1)
+        quantize(nc, x_codes[1], x_scales[1], x_grouped[1])
+        multiply(1)
+        finish(0, 2)
+        finish(0, 3)
+        for g in range(G):
+            finish(1, g)

@@ -17,7 +17,7 @@ PACK = 4
 ROWS = D // PACK
 HALF = N // 2
 MM_N = 128
-VECTOR_COLS = (144, 96)
+VECTOR_COLS = (144, 128)
 
 
 def interleave(copy, grouped, raw, cols):
@@ -56,7 +56,8 @@ def tile_rows_mix_sgu_kernel(tc, x, w, b, u, out):
         w_grouped = sb.tile([P, M, PACK], BF16, align_bytes=64)
         w_codes = sb.tile([P, M], U32, align_bytes=64)
         w_scales = sb.tile([P, M], U8, align_bytes=64)
-        bias = sb.tile([P, 1], F32)
+        bias_rows = sb.tile([P, ROWS], F32, align_bytes=64)
+        bias = sb.tile([P, ROWS], F32, align_bytes=64)
         gate = [[sb.tile([P, HALF], F32, name=f"gate{h}_{g}", align_bytes=64) for g in range(G)] for h in range(2)]
         result = [[sb.tile([P, HALF], F32, name=f"result{h}_{g}", align_bytes=64) for g in range(G)] for h in range(2)]
         z = [[ps.tile([P, HALF], F32, name=f"z{h}_{g}") for g in range(G)] for h in range(2)]
@@ -64,27 +65,29 @@ def tile_rows_mix_sgu_kernel(tc, x, w, b, u, out):
         for g in range(G):
             queue = nc.sync if g < 2 else nc.scalar
             queue.dma_start(out=w_raw[ROWS * g : ROWS * (g + 1)], in_=w_rows)
+        nc.vector.memset(bias_rows[:], 0.0)
+        nc.scalar.dma_start(out=bias_rows[0:P:ROWS, :], in_=b.rearrange("(q i) o -> q (i o)", i=ROWS))
         nc.sync.dma_start(out=x_raw[0][:], in_=x_rows[:, :, halves[0]])
         nc.sync.dma_start(out=x_raw[1][:], in_=x_rows[:, :, halves[1]])
-        nc.sync.dma_start(out=bias[:], in_=b)
         for h in range(2):
             for g in range(G):
                 nc.sync.dma_start(out=gate[h][g][:], in_=u_rows[:, g, halves[h]])
 
         def multiply(h):
-            for g in range(G):
-                rows = slice(ROWS * g, ROWS * (g + 1))
+            for pair in range(0, G, 2):
                 for c in range(0, HALF, MM_N):
                     cols = slice(c, c + MM_N)
-                    nc.tensor.matmul_mx(
-                        out=z[h][g][:, cols],
-                        lhsT=w_codes[rows, :].bitcast(FP8X4),
-                        lhsT_scale=w_scales[rows, :],
-                        rhs=x_codes[h][rows, cols].bitcast(FP8X4),
-                        rhs_scale=x_scales[h][rows, cols],
-                        start=True,
-                        stop=True,
-                    )
+                    for g in (pair, pair + 1):
+                        rows = slice(ROWS * g, ROWS * (g + 1))
+                        nc.tensor.matmul_mx(
+                            out=z[h][g][:, cols],
+                            lhsT=w_codes[rows, :].bitcast(FP8X4),
+                            lhsT_scale=w_scales[rows, :],
+                            rhs=x_codes[h][rows, cols].bitcast(FP8X4),
+                            rhs_scale=x_scales[h][rows, cols],
+                            start=True,
+                            stop=True,
+                        )
 
         def group_x(h):
             interleave(nc.vector.tensor_copy, x_grouped[h], x_raw[h], slice(0, VECTOR_COLS[h]))
@@ -104,13 +107,14 @@ def tile_rows_mix_sgu_kernel(tc, x, w, b, u, out):
         interleave(nc.vector.tensor_copy, w_grouped, w_raw, slice(0, M))
         quantize(nc, w_codes, w_scales, w_grouped)
         group_x(0)
+        nc.vector.transpose(out=bias[:], in_=bias_rows[:])
         quantize(nc, x_codes[0], x_scales[0], x_grouped[0])
         multiply(0)
         group_x(1)
         finish(0, 0)
-        finish(0, 1)
         quantize(nc, x_codes[1], x_scales[1], x_grouped[1])
         multiply(1)
+        finish(0, 1)
         finish(0, 2)
         finish(0, 3)
         for g in range(G):

@@ -11,13 +11,14 @@ U32 = mybir.dt.uint32
 U8 = mybir.dt.uint8
 FP8X4 = mybir.dt.float8_e4m3fn_x4
 ALU = mybir.AluOpType
+ACT = mybir.ActivationFunctionType
 
 P = 128
 PACK = 4
 ROWS = D // PACK
 HALF = N // 2
 MM_N = 128
-VECTOR_COLS = (144, 128)
+VECTOR_COLS = 128
 
 
 def interleave(copy, grouped, raw, cols):
@@ -27,11 +28,11 @@ def interleave(copy, grouped, raw, cols):
     )
 
 
-def quantize(nc, codes, scales, grouped):
+def quantize(nc, codes, scales, grouped, cols):
     nc.vector.quantize_mx(
-        out=codes[:].bitcast(FP8X4),
-        scales=scales[:],
-        in_=grouped[:].rearrange("p c j -> p (c j)"),
+        out=codes[:, cols].bitcast(FP8X4),
+        scales=scales[:, cols],
+        in_=grouped[:, cols, :].rearrange("p c j -> p (c j)"),
     )
 
 
@@ -39,9 +40,8 @@ def tile_rows_mix_sgu_kernel(tc, x, w, b, u, out):
     nc = tc.nc
     x_rows = x.rearrange("g (p j) n -> (g p) j n", j=PACK)
     w_rows = w.rearrange("(p j) m -> p j m", j=PACK)
-    u_rows = u.rearrange("g m n -> m g n")
-    out_rows = out.rearrange("g m n -> m g n")
     halves = [slice(h * HALF, (h + 1) * HALF) for h in range(2)]
+    blocks = [slice(c, c + MM_N) for c in range(0, HALF, MM_N)]
 
     with ExitStack() as ctx:
         sb = ctx.enter_context(tc.tile_pool(name="sb", bufs=1))
@@ -60,6 +60,7 @@ def tile_rows_mix_sgu_kernel(tc, x, w, b, u, out):
         bias = sb.tile([P, ROWS], F32, align_bytes=64)
         gate = [[sb.tile([P, HALF], F32, name=f"gate{h}_{g}", align_bytes=64) for g in range(G)] for h in range(2)]
         result = [[sb.tile([P, HALF], F32, name=f"result{h}_{g}", align_bytes=64) for g in range(G)] for h in range(2)]
+        biased = sb.tile([P, HALF], F32, align_bytes=64)
         z = [[ps.tile([P, HALF], F32, name=f"z{h}_{g}") for g in range(G)] for h in range(2)]
 
         for g in range(G):
@@ -67,31 +68,32 @@ def tile_rows_mix_sgu_kernel(tc, x, w, b, u, out):
             queue.dma_start(out=w_raw[ROWS * g : ROWS * (g + 1)], in_=w_rows)
         nc.vector.memset(bias_rows[:], 0.0)
         nc.scalar.dma_start(out=bias_rows[0:P:ROWS, :], in_=b.rearrange("(q i) o -> q (i o)", i=ROWS))
-        nc.sync.dma_start(out=x_raw[0][:], in_=x_rows[:, :, halves[0]])
-        nc.sync.dma_start(out=x_raw[1][:], in_=x_rows[:, :, halves[1]])
+        for h in range(2):
+            nc.sync.dma_start(out=x_raw[h][:], in_=x_rows[:, :, halves[h]])
         for h in range(2):
             for g in range(G):
-                nc.sync.dma_start(out=gate[h][g][:], in_=u_rows[:, g, halves[h]])
+                nc.sync.dma_start(out=gate[h][g][:], in_=u[g][:, halves[h]])
 
-        def multiply(h):
+        def multiply(h, g, cols):
+            rows = slice(ROWS * g, ROWS * (g + 1))
+            nc.tensor.matmul_mx(
+                out=z[h][g][:, cols],
+                lhsT=w_codes[rows, :].bitcast(FP8X4),
+                lhsT_scale=w_scales[rows, :],
+                rhs=x_codes[h][rows, cols].bitcast(FP8X4),
+                rhs_scale=x_scales[h][rows, cols],
+                start=True,
+                stop=True,
+            )
+
+        def multiply_half(h):
             for pair in range(0, G, 2):
-                for c in range(0, HALF, MM_N):
-                    cols = slice(c, c + MM_N)
+                for cols in blocks:
                     for g in (pair, pair + 1):
-                        rows = slice(ROWS * g, ROWS * (g + 1))
-                        nc.tensor.matmul_mx(
-                            out=z[h][g][:, cols],
-                            lhsT=w_codes[rows, :].bitcast(FP8X4),
-                            lhsT_scale=w_scales[rows, :],
-                            rhs=x_codes[h][rows, cols].bitcast(FP8X4),
-                            rhs_scale=x_scales[h][rows, cols],
-                            start=True,
-                            stop=True,
-                        )
+                        multiply(h, g, cols)
 
-        def group_x(h):
-            interleave(nc.vector.tensor_copy, x_grouped[h], x_raw[h], slice(0, VECTOR_COLS[h]))
-            interleave(nc.scalar.copy, x_grouped[h], x_raw[h], slice(VECTOR_COLS[h], HALF))
+        def store(h, g):
+            nc.sync.dma_start(out=out[g][:, halves[h]], in_=result[h][g][:])
 
         def finish(h, g):
             nc.vector.scalar_tensor_tensor(
@@ -102,20 +104,31 @@ def tile_rows_mix_sgu_kernel(tc, x, w, b, u, out):
                 op0=ALU.add,
                 op1=ALU.mult,
             )
-            nc.sync.dma_start(out=out_rows[:, g, halves[h]], in_=result[h][g][:])
+
+        def finish_aside(h, g):
+            nc.scalar.activation(out=biased[:], in_=z[h][g][:], func=ACT.Identity, bias=bias[:, 0:1], scale=1.0)
+            nc.gpsimd.tensor_tensor(out=result[h][g][:], in0=biased[:], in1=gate[h][g][:], op=ALU.mult)
 
         interleave(nc.vector.tensor_copy, w_grouped, w_raw, slice(0, M))
-        quantize(nc, w_codes, w_scales, w_grouped)
-        group_x(0)
+        quantize(nc, w_codes, w_scales, w_grouped, slice(0, M))
+        interleave(nc.vector.tensor_copy, x_grouped[0], x_raw[0], blocks[0])
+        interleave(nc.scalar.copy, x_grouped[0], x_raw[0], blocks[1])
         nc.vector.transpose(out=bias[:], in_=bias_rows[:])
-        quantize(nc, x_codes[0], x_scales[0], x_grouped[0])
-        multiply(0)
-        group_x(1)
+        for cols in blocks:
+            quantize(nc, x_codes[0], x_scales[0], x_grouped[0], cols)
+        multiply_half(0)
+        interleave(nc.vector.tensor_copy, x_grouped[1], x_raw[1], slice(0, VECTOR_COLS))
+        interleave(nc.scalar.copy, x_grouped[1], x_raw[1], slice(VECTOR_COLS, HALF))
         finish(0, 0)
-        quantize(nc, x_codes[1], x_scales[1], x_grouped[1])
-        multiply(1)
-        finish(0, 1)
-        finish(0, 2)
-        finish(0, 3)
+        store(0, 0)
+        finish_aside(0, 1)
+        for cols in blocks:
+            quantize(nc, x_codes[1], x_scales[1], x_grouped[1], cols)
+        multiply_half(1)
+        for g in (2, 3):
+            finish(0, g)
+            store(0, g)
+        store(0, 1)
         for g in range(G):
             finish(1, g)
+            store(1, g)

@@ -70,8 +70,8 @@ def tile_rows_mix_sgu_kernel(tc, x, w, b, u, out):
         nc.scalar.dma_start(out=bias_rows[0:P:ROWS, :], in_=b.rearrange("(q i) o -> q (i o)", i=ROWS))
         for h in range(2):
             nc.sync.dma_start(out=x_raw[h][:], in_=x_rows[:, :, halves[h]])
-        for h in range(2):
-            for g in range(G):
+        for h, order in enumerate(((0, 2, 3, 1), (0, 1, 2, 3))):
+            for g in order:
                 nc.sync.dma_start(out=gate[h][g][:], in_=u[g][:, halves[h]])
 
         def multiply(h, g, cols):

@@ -48,7 +48,8 @@ def tile_rows_mix_sgu_kernel(tc, x, w, b, u, out):
         ps = ctx.enter_context(tc.psum_pool(name="ps", bufs=1))
         ctx.enter_context(tc.manual_schedule())
 
-        x_raw = [sb.tile([P, PACK, HALF], F32, name=f"x_raw{h}", align_bytes=64) for h in range(2)]
+        x_first = [sb.tile([P, 2, HALF], F32, name=f"x_first{r}", align_bytes=64) for r in range(2)]
+        x_second = sb.tile([P, PACK, HALF], F32, align_bytes=64)
         x_grouped = [sb.tile([P, HALF, PACK], BF16, name=f"x_grouped{h}", align_bytes=64) for h in range(2)]
         x_codes = [sb.tile([P, HALF], U32, name=f"x_codes{h}", align_bytes=64) for h in range(2)]
         x_scales = [sb.tile([P, HALF], U8, name=f"x_scales{h}", align_bytes=64) for h in range(2)]
@@ -59,7 +60,11 @@ def tile_rows_mix_sgu_kernel(tc, x, w, b, u, out):
         bias_rows = sb.tile([P, ROWS], F32, align_bytes=64)
         bias = sb.tile([P, ROWS], F32, align_bytes=64)
         gate = [[sb.tile([P, HALF], F32, name=f"gate{h}_{g}", align_bytes=64) for g in range(G)] for h in range(2)]
-        result = [[sb.tile([P, HALF], F32, name=f"result{h}_{g}", align_bytes=64) for g in range(G)] for h in range(2)]
+        result_last = sb.tile([P, N], F32, align_bytes=64)
+        result = [
+            [sb.tile([P, HALF], F32, name=f"result{h}_{g}", align_bytes=64)[:] for g in range(G - 1)] + [result_last[:, halves[h]]]
+            for h in range(2)
+        ]
         biased = sb.tile([P, HALF], F32, align_bytes=64)
         z = [[ps.tile([P, HALF], F32, name=f"z{h}_{g}") for g in range(G)] for h in range(2)]
 
@@ -68,9 +73,10 @@ def tile_rows_mix_sgu_kernel(tc, x, w, b, u, out):
             queue.dma_start(out=w_raw[ROWS * g : ROWS * (g + 1)], in_=w_rows)
         nc.vector.memset(bias_rows[:], 0.0)
         nc.scalar.dma_start(out=bias_rows[0:P:ROWS, :], in_=b.rearrange("(q i) o -> q (i o)", i=ROWS))
-        for h in range(2):
-            nc.sync.dma_start(out=x_raw[h][:], in_=x_rows[:, :, halves[h]])
-        for h, order in enumerate(((0, 2, 3, 1), (0, 1, 2, 3))):
+        for r in range(2):
+            nc.sync.dma_start(out=x_first[r][:], in_=x_rows[:, 2 * r : 2 * r + 2, halves[0]])
+        nc.sync.dma_start(out=x_second[:], in_=x_rows[:, :, halves[1]])
+        for h, order in enumerate(((0, 2, 1, 3), (0, 1, 2, 3))):
             for g in order:
                 nc.sync.dma_start(out=gate[h][g][:], in_=u[g][:, halves[h]])
 
@@ -86,18 +92,12 @@ def tile_rows_mix_sgu_kernel(tc, x, w, b, u, out):
                 stop=True,
             )
 
-        def multiply_half(h):
-            for pair in range(0, G, 2):
-                for cols in blocks:
-                    for g in (pair, pair + 1):
-                        multiply(h, g, cols)
-
         def store(h, g):
-            nc.sync.dma_start(out=out[g][:, halves[h]], in_=result[h][g][:])
+            nc.sync.dma_start(out=out[g][:, halves[h]], in_=result[h][g])
 
         def finish(h, g):
             nc.vector.scalar_tensor_tensor(
-                out=result[h][g][:],
+                out=result[h][g],
                 in0=z[h][g][:],
                 scalar=bias[:, 0:1],
                 in1=gate[h][g][:],
@@ -107,28 +107,37 @@ def tile_rows_mix_sgu_kernel(tc, x, w, b, u, out):
 
         def finish_aside(h, g):
             nc.scalar.activation(out=biased[:], in_=z[h][g][:], func=ACT.Identity, bias=bias[:, 0:1], scale=1.0)
-            nc.gpsimd.tensor_tensor(out=result[h][g][:], in0=biased[:], in1=gate[h][g][:], op=ALU.mult)
+            nc.gpsimd.tensor_tensor(out=result[h][g], in0=biased[:], in1=gate[h][g][:], op=ALU.mult)
 
         interleave(nc.vector.tensor_copy, w_grouped, w_raw, slice(0, M))
-        quantize(nc, w_codes, w_scales, w_grouped, slice(0, M))
-        interleave(nc.vector.tensor_copy, x_grouped[0], x_raw[0], blocks[0])
-        interleave(nc.scalar.copy, x_grouped[0], x_raw[0], blocks[1])
+        for r in range(2):
+            interleave(nc.vector.tensor_copy, x_grouped[0][:, :, 2 * r : 2 * r + 2], x_first[r], blocks[0])
+            interleave(nc.scalar.copy, x_grouped[0][:, :, 2 * r : 2 * r + 2], x_first[r], blocks[1])
+            if r == 0:
+                quantize(nc, w_codes, w_scales, w_grouped, slice(0, M))
         nc.vector.transpose(out=bias[:], in_=bias_rows[:])
         for cols in blocks:
             quantize(nc, x_codes[0], x_scales[0], x_grouped[0], cols)
-        multiply_half(0)
-        interleave(nc.vector.tensor_copy, x_grouped[1], x_raw[1], slice(0, VECTOR_COLS))
-        interleave(nc.scalar.copy, x_grouped[1], x_raw[1], slice(VECTOR_COLS, HALF))
+        for pair in range(0, G, 2):
+            for cols in blocks:
+                for g in (pair, pair + 1):
+                    multiply(0, g, cols)
+        interleave(nc.vector.tensor_copy, x_grouped[1], x_second, slice(0, VECTOR_COLS))
+        interleave(nc.scalar.copy, x_grouped[1], x_second, slice(VECTOR_COLS, HALF))
         finish(0, 0)
         store(0, 0)
         finish_aside(0, 1)
         for cols in blocks:
             quantize(nc, x_codes[1], x_scales[1], x_grouped[1], cols)
-        multiply_half(1)
-        for g in (2, 3):
-            finish(0, g)
-            store(0, g)
-        store(0, 1)
         for g in range(G):
+            for cols in blocks:
+                multiply(1, g, cols)
+        finish(0, 2)
+        store(0, 2)
+        store(0, 1)
+        finish(0, 3)
+        for g in range(G - 1):
             finish(1, g)
             store(1, g)
+        finish(1, 3)
+        nc.sync.dma_start(out=out[3], in_=result_last[:])

@@ -60,11 +60,7 @@ def tile_rows_mix_sgu_kernel(tc, x, w, b, u, out):
         bias_rows = sb.tile([P, ROWS], F32, align_bytes=64)
         bias = sb.tile([P, ROWS], F32, align_bytes=64)
         gate = [[sb.tile([P, HALF], F32, name=f"gate{h}_{g}", align_bytes=64) for g in range(G)] for h in range(2)]
-        result_last = sb.tile([P, N], F32, align_bytes=64)
-        result = [
-            [sb.tile([P, HALF], F32, name=f"result{h}_{g}", align_bytes=64)[:] for g in range(G - 1)] + [result_last[:, halves[h]]]
-            for h in range(2)
-        ]
+        result = [[sb.tile([P, HALF], F32, name=f"result{h}_{g}", align_bytes=64)[:] for g in range(G)] for h in range(2)]
         biased = sb.tile([P, HALF], F32, align_bytes=64)
         z = [[ps.tile([P, HALF], F32, name=f"z{h}_{g}") for g in range(G)] for h in range(2)]
 
@@ -132,12 +128,10 @@ def tile_rows_mix_sgu_kernel(tc, x, w, b, u, out):
         for g in range(G):
             for cols in blocks:
                 multiply(1, g, cols)
-        finish(0, 2)
-        store(0, 2)
+        for g in (2, 3):
+            finish(0, g)
+            store(0, g)
         store(0, 1)
-        finish(0, 3)
-        for g in range(G - 1):
+        for g in range(G):
             finish(1, g)
             store(1, g)
-        finish(1, 3)
-        nc.sync.dma_start(out=out[3], in_=result_last[:])

@@ -11,7 +11,6 @@ U32 = mybir.dt.uint32
 U8 = mybir.dt.uint8
 FP8X4 = mybir.dt.float8_e4m3fn_x4
 ALU = mybir.AluOpType
-ACT = mybir.ActivationFunctionType
 
 P = 128
 PACK = 4
@@ -61,7 +60,6 @@ def tile_rows_mix_sgu_kernel(tc, x, w, b, u, out):
         bias = sb.tile([P, ROWS], F32, align_bytes=64)
         gate = [[sb.tile([P, HALF], F32, name=f"gate{h}_{g}", align_bytes=64) for g in range(G)] for h in range(2)]
         result = [[sb.tile([P, HALF], F32, name=f"result{h}_{g}", align_bytes=64)[:] for g in range(G)] for h in range(2)]
-        biased = sb.tile([P, HALF], F32, align_bytes=64)
         z = [[ps.tile([P, HALF], F32, name=f"z{h}_{g}") for g in range(G)] for h in range(2)]
 
         for g in range(G):
@@ -72,8 +70,8 @@ def tile_rows_mix_sgu_kernel(tc, x, w, b, u, out):
         for r in range(2):
             nc.sync.dma_start(out=x_first[r][:], in_=x_rows[:, 2 * r : 2 * r + 2, halves[0]])
         nc.sync.dma_start(out=x_second[:], in_=x_rows[:, :, halves[1]])
-        for h, order in enumerate(((0, 2, 1, 3), (0, 1, 2, 3))):
-            for g in order:
+        for h in range(2):
+            for g in range(G):
                 nc.sync.dma_start(out=gate[h][g][:], in_=u[g][:, halves[h]])
 
         def multiply(h, g, cols):
@@ -101,10 +99,6 @@ def tile_rows_mix_sgu_kernel(tc, x, w, b, u, out):
                 op1=ALU.mult,
             )
 
-        def finish_aside(h, g):
-            nc.scalar.activation(out=biased[:], in_=z[h][g][:], func=ACT.Identity, bias=bias[:, 0:1], scale=1.0)
-            nc.gpsimd.tensor_tensor(out=result[h][g], in0=biased[:], in1=gate[h][g][:], op=ALU.mult)
-
         interleave(nc.vector.tensor_copy, w_grouped, w_raw, slice(0, M))
         for r in range(2):
             interleave(nc.vector.tensor_copy, x_grouped[0][:, :, 2 * r : 2 * r + 2], x_first[r], blocks[0])
@@ -122,16 +116,14 @@ def tile_rows_mix_sgu_kernel(tc, x, w, b, u, out):
         interleave(nc.scalar.copy, x_grouped[1], x_second, slice(VECTOR_COLS, HALF))
         finish(0, 0)
         store(0, 0)
-        finish_aside(0, 1)
         for cols in blocks:
             quantize(nc, x_codes[1], x_scales[1], x_grouped[1], cols)
         for g in range(G):
             for cols in blocks:
                 multiply(1, g, cols)
-        for g in (2, 3):
+        for g in (1, 2, 3):
             finish(0, g)
             store(0, g)
-        store(0, 1)
         for g in range(G):
             finish(1, g)
             store(1, g)

@@ -17,7 +17,6 @@ PACK = 4
 ROWS = D // PACK
 HALF = N // 2
 MM_N = 128
-VECTOR_COLS = 128
 
 
 def interleave(copy, grouped, raw, cols):
@@ -47,8 +46,7 @@ def tile_rows_mix_sgu_kernel(tc, x, w, b, u, out):
         ps = ctx.enter_context(tc.psum_pool(name="ps", bufs=1))
         ctx.enter_context(tc.manual_schedule())
 
-        x_first = [sb.tile([P, 2, HALF], F32, name=f"x_first{r}", align_bytes=64) for r in range(2)]
-        x_second = sb.tile([P, PACK, HALF], F32, align_bytes=64)
+        x_raw = [[sb.tile([P, 2, HALF], F32, name=f"x_raw{h}_{r}", align_bytes=64) for r in range(2)] for h in range(2)]
         x_grouped = [sb.tile([P, HALF, PACK], BF16, name=f"x_grouped{h}", align_bytes=64) for h in range(2)]
         x_codes = [sb.tile([P, HALF], U32, name=f"x_codes{h}", align_bytes=64) for h in range(2)]
         x_scales = [sb.tile([P, HALF], U8, name=f"x_scales{h}", align_bytes=64) for h in range(2)]
@@ -58,7 +56,9 @@ def tile_rows_mix_sgu_kernel(tc, x, w, b, u, out):
         w_scales = sb.tile([P, M], U8, align_bytes=64)
         bias_rows = sb.tile([P, ROWS], F32, align_bytes=64)
         bias = sb.tile([P, ROWS], F32, align_bytes=64)
-        gate = [[sb.tile([P, HALF], F32, name=f"gate{h}_{g}", align_bytes=64) for g in range(G)] for h in range(2)]
+        gate = [[sb.tile([P, HALF], F32, name=f"gate{h}_{g}", align_bytes=64)[:] for g in range(G)] for h in range(2)]
+        gate_pair = sb.tile([P, 2, HALF], F32, align_bytes=64)
+        gate[0][2], gate[0][3] = gate_pair[:, 0, :], gate_pair[:, 1, :]
         result = [[sb.tile([P, HALF], F32, name=f"result{h}_{g}", align_bytes=64)[:] for g in range(G)] for h in range(2)]
         z = [[ps.tile([P, HALF], F32, name=f"z{h}_{g}") for g in range(G)] for h in range(2)]
 
@@ -67,12 +67,14 @@ def tile_rows_mix_sgu_kernel(tc, x, w, b, u, out):
             queue.dma_start(out=w_raw[ROWS * g : ROWS * (g + 1)], in_=w_rows)
         nc.vector.memset(bias_rows[:], 0.0)
         nc.scalar.dma_start(out=bias_rows[0:P:ROWS, :], in_=b.rearrange("(q i) o -> q (i o)", i=ROWS))
-        for r in range(2):
-            nc.sync.dma_start(out=x_first[r][:], in_=x_rows[:, 2 * r : 2 * r + 2, halves[0]])
-        nc.sync.dma_start(out=x_second[:], in_=x_rows[:, :, halves[1]])
         for h in range(2):
-            for g in range(G):
-                nc.sync.dma_start(out=gate[h][g][:], in_=u[g][:, halves[h]])
+            for r in range(2):
+                nc.sync.dma_start(out=x_raw[h][r][:], in_=x_rows[:, 2 * r : 2 * r + 2, halves[h]])
+        for g in (0, 1):
+            nc.sync.dma_start(out=gate[0][g], in_=u[g][:, halves[0]])
+        nc.sync.dma_start(out=gate_pair[:], in_=u.rearrange("g m n -> m g n")[:, 2:G, halves[0]])
+        for g in range(G):
+            nc.sync.dma_start(out=gate[1][g], in_=u[g][:, halves[1]])
 
         def multiply(h, g, cols):
             rows = slice(ROWS * g, ROWS * (g + 1))
@@ -94,36 +96,43 @@ def tile_rows_mix_sgu_kernel(tc, x, w, b, u, out):
                 out=result[h][g],
                 in0=z[h][g][:],
                 scalar=bias[:, 0:1],
-                in1=gate[h][g][:],
+                in1=gate[h][g],
                 op0=ALU.add,
                 op1=ALU.mult,
             )
 
+        def multiply_skewed(h, samples):
+            for step in range(len(samples) + 1):
+                if step < len(samples):
+                    multiply(h, samples[step], blocks[0])
+                if step > 0:
+                    multiply(h, samples[step - 1], blocks[1])
+
+        def cast(h, r):
+            places = x_grouped[h][:, :, 2 * r : 2 * r + 2]
+            interleave(nc.vector.tensor_copy, places, x_raw[h][r], blocks[0])
+            interleave(nc.scalar.copy, places, x_raw[h][r], blocks[1])
+
         interleave(nc.vector.tensor_copy, w_grouped, w_raw, slice(0, M))
-        for r in range(2):
-            interleave(nc.vector.tensor_copy, x_grouped[0][:, :, 2 * r : 2 * r + 2], x_first[r], blocks[0])
-            interleave(nc.scalar.copy, x_grouped[0][:, :, 2 * r : 2 * r + 2], x_first[r], blocks[1])
-            if r == 0:
-                quantize(nc, w_codes, w_scales, w_grouped, slice(0, M))
-        nc.vector.transpose(out=bias[:], in_=bias_rows[:])
+        cast(0, 0)
+        quantize(nc, w_codes, w_scales, w_grouped, slice(0, M))
+        places = x_grouped[0][:, :, 2:4]
+        interleave(nc.vector.tensor_copy, places, x_raw[0][1], slice(0, MM_N // 2))
+        interleave(nc.scalar.copy, places, x_raw[0][1], slice(MM_N // 2, MM_N))
+        interleave(nc.vector.tensor_copy, places, x_raw[0][1], blocks[1])
         for cols in blocks:
             quantize(nc, x_codes[0], x_scales[0], x_grouped[0], cols)
-        for pair in range(0, G, 2):
-            for cols in blocks:
-                for g in (pair, pair + 1):
-                    multiply(0, g, cols)
-        interleave(nc.vector.tensor_copy, x_grouped[1], x_second, slice(0, VECTOR_COLS))
-        interleave(nc.scalar.copy, x_grouped[1], x_second, slice(VECTOR_COLS, HALF))
+        nc.vector.transpose(out=bias[:], in_=bias_rows[:])
+        for cols in blocks:
+            multiply(0, 0, cols)
+        multiply_skewed(0, range(1, G))
+        cast(1, 0)
+        cast(1, 1)
         finish(0, 0)
         store(0, 0)
         for cols in blocks:
             quantize(nc, x_codes[1], x_scales[1], x_grouped[1], cols)
-        for g in range(G):
-            for cols in blocks:
-                multiply(1, g, cols)
-        for g in (1, 2, 3):
-            finish(0, g)
-            store(0, g)
-        for g in range(G):
-            finish(1, g)
-            store(1, g)
+        multiply_skewed(1, range(G))
+        for h, g in [(0, 1), (0, 2), (0, 3)] + [(1, g) for g in range(G)]:
+            finish(h, g)
+            store(h, g)

@@ -40,6 +40,7 @@ def tile_rows_mix_sgu_kernel(tc, x, w, b, u, out):
     w_rows = w.rearrange("(p j) m -> p j m", j=PACK)
     halves = [slice(h * HALF, (h + 1) * HALF) for h in range(2)]
     blocks = [slice(c, c + MM_N) for c in range(0, HALF, MM_N)]
+    pairs = [slice(0, 2), slice(2, 4)]
 
     with ExitStack() as ctx:
         sb = ctx.enter_context(tc.tile_pool(name="sb", bufs=1))
@@ -56,10 +57,11 @@ def tile_rows_mix_sgu_kernel(tc, x, w, b, u, out):
         w_scales = sb.tile([P, M], U8, align_bytes=64)
         bias_rows = sb.tile([P, ROWS], F32, align_bytes=64)
         bias = sb.tile([P, ROWS], F32, align_bytes=64)
-        gate = [[sb.tile([P, HALF], F32, name=f"gate{h}_{g}", align_bytes=64)[:] for g in range(G)] for h in range(2)]
-        gate_pair = sb.tile([P, 2, HALF], F32, align_bytes=64)
-        gate[0][2], gate[0][3] = gate_pair[:, 0, :], gate_pair[:, 1, :]
-        result = [[sb.tile([P, HALF], F32, name=f"result{h}_{g}", align_bytes=64)[:] for g in range(G)] for h in range(2)]
+        alone = [(0, 0), (0, 1)] + [(1, g) for g in range(G)]
+        gate = {(h, g): sb.tile([P, HALF], F32, name=f"gate{h}_{g}", align_bytes=64)[:] for h, g in alone}
+        gate_joined = sb.tile([P, 2, HALF], F32, align_bytes=64)
+        gate[0, 2], gate[0, 3] = gate_joined[:, 0, :], gate_joined[:, 1, :]
+        result = [[sb.tile([P, HALF], F32, name=f"result{h}_{g}", align_bytes=64) for g in range(G)] for h in range(2)]
         z = [[ps.tile([P, HALF], F32, name=f"z{h}_{g}") for g in range(G)] for h in range(2)]
 
         for g in range(G):
@@ -69,12 +71,19 @@ def tile_rows_mix_sgu_kernel(tc, x, w, b, u, out):
         nc.scalar.dma_start(out=bias_rows[0:P:ROWS, :], in_=b.rearrange("(q i) o -> q (i o)", i=ROWS))
         for h in range(2):
             for r in range(2):
-                nc.sync.dma_start(out=x_raw[h][r][:], in_=x_rows[:, 2 * r : 2 * r + 2, halves[h]])
+                nc.sync.dma_start(out=x_raw[h][r][:], in_=x_rows[:, pairs[r], halves[h]])
         for g in (0, 1):
-            nc.sync.dma_start(out=gate[0][g], in_=u[g][:, halves[0]])
-        nc.sync.dma_start(out=gate_pair[:], in_=u.rearrange("g m n -> m g n")[:, 2:G, halves[0]])
+            nc.sync.dma_start(out=gate[0, g], in_=u[g][:, halves[0]])
+        nc.sync.dma_start(out=gate_joined[:], in_=u.rearrange("g m n -> m g n")[:, 2:G, halves[0]])
         for g in range(G):
-            nc.sync.dma_start(out=gate[1][g], in_=u[g][:, halves[1]])
+            nc.sync.dma_start(out=gate[1, g], in_=u[g][:, halves[1]])
+
+        def cast(copy, h, r, cols):
+            interleave(copy, x_grouped[h][:, :, pairs[r]], x_raw[h][r], cols)
+
+        def cast_shared(h, r):
+            cast(nc.vector.tensor_copy, h, r, blocks[0])
+            cast(nc.scalar.copy, h, r, blocks[1])
 
         def multiply(h, g, cols):
             rows = slice(ROWS * g, ROWS * (g + 1))
@@ -88,19 +97,6 @@ def tile_rows_mix_sgu_kernel(tc, x, w, b, u, out):
                 stop=True,
             )
 
-        def store(h, g):
-            nc.sync.dma_start(out=out[g][:, halves[h]], in_=result[h][g])
-
-        def finish(h, g):
-            nc.vector.scalar_tensor_tensor(
-                out=result[h][g],
-                in0=z[h][g][:],
-                scalar=bias[:, 0:1],
-                in1=gate[h][g],
-                op0=ALU.add,
-                op1=ALU.mult,
-            )
-
         def multiply_skewed(h, samples):
             for step in range(len(samples) + 1):
                 if step < len(samples):
@@ -108,31 +104,36 @@ def tile_rows_mix_sgu_kernel(tc, x, w, b, u, out):
                 if step > 0:
                     multiply(h, samples[step - 1], blocks[1])
 
-        def cast(h, r):
-            places = x_grouped[h][:, :, 2 * r : 2 * r + 2]
-            interleave(nc.vector.tensor_copy, places, x_raw[h][r], blocks[0])
-            interleave(nc.scalar.copy, places, x_raw[h][r], blocks[1])
+        def finish(h, g):
+            nc.vector.scalar_tensor_tensor(
+                out=result[h][g][:],
+                in0=z[h][g][:],
+                scalar=bias[:, 0:1],
+                in1=gate[h, g],
+                op0=ALU.add,
+                op1=ALU.mult,
+            )
+            nc.sync.dma_start(out=out[g][:, halves[h]], in_=result[h][g][:])
 
         interleave(nc.vector.tensor_copy, w_grouped, w_raw, slice(0, M))
-        cast(0, 0)
+        cast_shared(0, 0)
         quantize(nc, w_codes, w_scales, w_grouped, slice(0, M))
-        places = x_grouped[0][:, :, 2:4]
-        interleave(nc.vector.tensor_copy, places, x_raw[0][1], slice(0, MM_N // 2))
-        interleave(nc.scalar.copy, places, x_raw[0][1], slice(MM_N // 2, MM_N))
-        interleave(nc.vector.tensor_copy, places, x_raw[0][1], blocks[1])
+
+        cast(nc.vector.tensor_copy, 0, 1, slice(0, MM_N // 2))
+        cast(nc.scalar.copy, 0, 1, slice(MM_N // 2, MM_N))
+        cast(nc.vector.tensor_copy, 0, 1, blocks[1])
         for cols in blocks:
             quantize(nc, x_codes[0], x_scales[0], x_grouped[0], cols)
         nc.vector.transpose(out=bias[:], in_=bias_rows[:])
         for cols in blocks:
             multiply(0, 0, cols)
         multiply_skewed(0, range(1, G))
-        cast(1, 0)
-        cast(1, 1)
+
+        for r in range(2):
+            cast_shared(1, r)
         finish(0, 0)
-        store(0, 0)
         for cols in blocks:
             quantize(nc, x_codes[1], x_scales[1], x_grouped[1], cols)
         multiply_skewed(1, range(G))
-        for h, g in [(0, 1), (0, 2), (0, 3)] + [(1, g) for g in range(G)]:
+        for h, g in [(0, g) for g in range(1, G)] + [(1, g) for g in range(G)]:
             finish(h, g)
-            store(h, g)

@@ -8,6 +8,7 @@ FLOPS = 2 * G * D * M * N
 F32 = mybir.dt.float32
 BF16 = mybir.dt.bfloat16
 U32 = mybir.dt.uint32
+I32 = mybir.dt.int32
 U8 = mybir.dt.uint8
 FP8X4 = mybir.dt.float8_e4m3fn_x4
 ALU = mybir.AluOpType
@@ -51,10 +52,9 @@ def tile_rows_mix_sgu_kernel(tc, x, w, b, u, out):
         x_grouped = [sb.tile([P, HALF, PACK], BF16, name=f"x_grouped{h}", align_bytes=64) for h in range(2)]
         x_codes = [sb.tile([P, HALF], U32, name=f"x_codes{h}", align_bytes=64) for h in range(2)]
         x_scales = [sb.tile([P, HALF], U8, name=f"x_scales{h}", align_bytes=64) for h in range(2)]
-        w_raw = sb.tile([P, PACK, M], F32, align_bytes=64)
-        w_grouped = sb.tile([P, M, PACK], BF16, align_bytes=64)
-        w_codes = sb.tile([P, M], U32, align_bytes=64)
-        w_scales = sb.tile([P, M], U8, align_bytes=64)
+        w_raw = sb.tile([ROWS, PACK, M], F32, align_bytes=64)
+        w_grouped = sb.tile([ROWS, M, PACK], BF16, align_bytes=64)
+        w_mx = [sb.tile([ROWS * (g + 1), M + M // 4], I32, name=f"w_mx{g}", align_bytes=64) for g in range(G)]
         bias_rows = sb.tile([P, ROWS], F32, align_bytes=64)
         bias = sb.tile([P, ROWS], F32, align_bytes=64)
         alone = [(0, 0), (0, 1)] + [(1, g) for g in range(G)]
@@ -64,16 +64,24 @@ def tile_rows_mix_sgu_kernel(tc, x, w, b, u, out):
         result = [[sb.tile([P, HALF], F32, name=f"result{h}_{g}", align_bytes=64) for g in range(G)] for h in range(2)]
         z = [[ps.tile([P, HALF], F32, name=f"z{h}_{g}") for g in range(G)] for h in range(2)]
 
-        for g in range(G):
-            queue = nc.sync if g < 2 else nc.scalar
-            queue.dma_start(out=w_raw[ROWS * g : ROWS * (g + 1)], in_=w_rows)
+        nc.sync.dma_start(out=w_raw[:], in_=w_rows)
         nc.vector.memset(bias_rows[:], 0.0)
-        nc.scalar.dma_start(out=bias_rows[0:P:ROWS, :], in_=b.rearrange("(q i) o -> q (i o)", i=ROWS))
+        nc.vector.memset(w_mx[0][:, M:], 0)
         for h in range(2):
             for r in range(2):
                 nc.sync.dma_start(out=x_raw[h][r][:], in_=x_rows[:, pairs[r], halves[h]])
-        for g in (0, 1):
-            nc.sync.dma_start(out=gate[0, g], in_=u[g][:, halves[0]])
+                if (h, r) == (0, 0):
+                    nc.sync.dma_start(out=bias_rows[0:P:ROWS, :], in_=b.rearrange("(q i) o -> q (i o)", i=ROWS))
+        nc.sync.dma_start(out=gate[0, 0], in_=u[0][:, halves[0]])
+        interleave(nc.vector.tensor_copy, w_grouped, w_raw, slice(0, M))
+        nc.vector.quantize_mx(
+            out=w_mx[0][:, 0:M].bitcast(FP8X4),
+            scales=w_mx[0][:, M:].bitcast(U8),
+            in_=w_grouped[:].rearrange("p c j -> p (c j)"),
+        )
+        for g in range(1, G):
+            nc.sync.dma_start(out=w_mx[g][ROWS * g :], in_=w_mx[0][:])
+        nc.sync.dma_start(out=gate[0, 1], in_=u[1][:, halves[0]])
         nc.sync.dma_start(out=gate_joined[:], in_=u.rearrange("g m n -> m g n")[:, 2:G, halves[0]])
         for g in range(G):
             nc.sync.dma_start(out=gate[1, g], in_=u[g][:, halves[1]])
@@ -89,8 +97,8 @@ def tile_rows_mix_sgu_kernel(tc, x, w, b, u, out):
             rows = slice(ROWS * g, ROWS * (g + 1))
             nc.tensor.matmul_mx(
                 out=z[h][g][:, cols],
-                lhsT=w_codes[rows, :].bitcast(FP8X4),
-                lhsT_scale=w_scales[rows, :],
+                lhsT=w_mx[g][rows, 0:M].bitcast(FP8X4),
+                lhsT_scale=w_mx[g][rows, M:].bitcast(U8),
                 rhs=x_codes[h][rows, cols].bitcast(FP8X4),
                 rhs_scale=x_scales[h][rows, cols],
                 start=True,
@@ -115,9 +123,7 @@ def tile_rows_mix_sgu_kernel(tc, x, w, b, u, out):
             )
             nc.sync.dma_start(out=out[g][:, halves[h]], in_=result[h][g][:])
 
-        interleave(nc.vector.tensor_copy, w_grouped, w_raw, slice(0, M))
         cast_shared(0, 0)
-        quantize(nc, w_codes, w_scales, w_grouped, slice(0, M))
 
         cast(nc.vector.tensor_copy, 0, 1, slice(0, MM_N // 2))
         cast(nc.scalar.copy, 0, 1, slice(MM_N // 2, MM_N))

from contextlib import ExitStack

import concourse.mybir as mybir

G, D, M, N = 4, 128, 128, 512
FLOPS = 2 * G * D * M * N

F32 = mybir.dt.float32
BF16 = mybir.dt.bfloat16
U32 = mybir.dt.uint32
I32 = mybir.dt.int32
U8 = mybir.dt.uint8
FP8X4 = mybir.dt.float8_e4m3fn_x4
ALU = mybir.AluOpType

P = 128
PACK = 4
ROWS = D // PACK
HALF = N // 2
MM_N = 128


def interleave(copy, grouped, raw, cols):
    copy(
        out=grouped[:, cols, :].rearrange("p (c i) j -> p c j i", i=4),
        in_=raw[:, :, cols].rearrange("p j (c i) -> p c j i", i=4),
    )


def quantize(nc, codes, scales, grouped, cols):
    nc.vector.quantize_mx(
        out=codes[:, cols].bitcast(FP8X4),
        scales=scales[:, cols],
        in_=grouped[:, cols, :].rearrange("p c j -> p (c j)"),
    )


def tile_rows_mix_sgu_kernel(tc, x, w, b, u, out):
    nc = tc.nc
    x_rows = x.rearrange("g (p j) n -> (g p) j n", j=PACK)
    w_rows = w.rearrange("(p j) m -> p j m", j=PACK)
    halves = [slice(h * HALF, (h + 1) * HALF) for h in range(2)]
    blocks = [slice(c, c + MM_N) for c in range(0, HALF, MM_N)]
    pairs = [slice(0, 2), slice(2, 4)]

    with ExitStack() as ctx:
        sb = ctx.enter_context(tc.tile_pool(name="sb", bufs=1))
        ps = ctx.enter_context(tc.psum_pool(name="ps", bufs=1))
        ctx.enter_context(tc.manual_schedule())

        x_raw = [[sb.tile([P, 2, HALF], F32, name=f"x_raw{h}_{r}", align_bytes=64) for r in range(2)] for h in range(2)]
        x_grouped = [sb.tile([P, HALF, PACK], BF16, name=f"x_grouped{h}", align_bytes=64) for h in range(2)]
        x_codes = [sb.tile([P, HALF], U32, name=f"x_codes{h}", align_bytes=64) for h in range(2)]
        x_scales = [sb.tile([P, HALF], U8, name=f"x_scales{h}", align_bytes=64) for h in range(2)]
        w_raw = sb.tile([ROWS, PACK, M], F32, align_bytes=64)
        w_grouped = sb.tile([ROWS, M, PACK], BF16, align_bytes=64)
        w_mx = [sb.tile([ROWS * (g + 1), M + M // 4], I32, name=f"w_mx{g}", align_bytes=64) for g in range(G)]
        bias_rows = sb.tile([P, ROWS], F32, align_bytes=64)
        bias = sb.tile([P, ROWS], F32, align_bytes=64)
        alone = [(0, 0), (0, 1)] + [(1, g) for g in range(G)]
        gate = {(h, g): sb.tile([P, HALF], F32, name=f"gate{h}_{g}", align_bytes=64)[:] for h, g in alone}
        gate_joined = sb.tile([P, 2, HALF], F32, align_bytes=64)
        gate[0, 2], gate[0, 3] = gate_joined[:, 0, :], gate_joined[:, 1, :]
        result = [[sb.tile([P, HALF], F32, name=f"result{h}_{g}", align_bytes=64) for g in range(G)] for h in range(2)]
        z = [[ps.tile([P, HALF], F32, name=f"z{h}_{g}") for g in range(G)] for h in range(2)]

        nc.sync.dma_start(out=w_raw[:], in_=w_rows)
        nc.vector.memset(bias_rows[:], 0.0)
        nc.vector.memset(w_mx[0][:, M:], 0)
        for h in range(2):
            for r in range(2):
                nc.sync.dma_start(out=x_raw[h][r][:], in_=x_rows[:, pairs[r], halves[h]])
                if (h, r) == (0, 0):
                    nc.sync.dma_start(out=bias_rows[0:P:ROWS, :], in_=b.rearrange("(q i) o -> q (i o)", i=ROWS))
        nc.sync.dma_start(out=gate[0, 0], in_=u[0][:, halves[0]])
        interleave(nc.vector.tensor_copy, w_grouped, w_raw, slice(0, M))
        nc.vector.quantize_mx(
            out=w_mx[0][:, 0:M].bitcast(FP8X4),
            scales=w_mx[0][:, M:].bitcast(U8),
            in_=w_grouped[:].rearrange("p c j -> p (c j)"),
        )
        for g in range(1, G):
            nc.sync.dma_start(out=w_mx[g][ROWS * g :], in_=w_mx[0][:])
        nc.sync.dma_start(out=gate[0, 1], in_=u[1][:, halves[0]])
        nc.sync.dma_start(out=gate_joined[:], in_=u.rearrange("g m n -> m g n")[:, 2:G, halves[0]])
        for g in range(G):
            nc.sync.dma_start(out=gate[1, g], in_=u[g][:, halves[1]])

        def cast(copy, h, r, cols):
            interleave(copy, x_grouped[h][:, :, pairs[r]], x_raw[h][r], cols)

        def cast_shared(h, r):
            cast(nc.vector.tensor_copy, h, r, blocks[0])
            cast(nc.scalar.copy, h, r, blocks[1])

        def multiply(h, g, cols):
            rows = slice(ROWS * g, ROWS * (g + 1))
            nc.tensor.matmul_mx(
                out=z[h][g][:, cols],
                lhsT=w_mx[g][rows, 0:M].bitcast(FP8X4),
                lhsT_scale=w_mx[g][rows, M:].bitcast(U8),
                rhs=x_codes[h][rows, cols].bitcast(FP8X4),
                rhs_scale=x_scales[h][rows, cols],
                start=True,
                stop=True,
            )

        def multiply_skewed(h, samples):
            for step in range(len(samples) + 1):
                if step < len(samples):
                    multiply(h, samples[step], blocks[0])
                if step > 0:
                    multiply(h, samples[step - 1], blocks[1])

        def finish(h, g):
            nc.vector.scalar_tensor_tensor(
                out=result[h][g][:],
                in0=z[h][g][:],
                scalar=bias[:, 0:1],
                in1=gate[h, g],
                op0=ALU.add,
                op1=ALU.mult,
            )
            nc.sync.dma_start(out=out[g][:, halves[h]], in_=result[h][g][:])

        cast_shared(0, 0)

        cast(nc.vector.tensor_copy, 0, 1, slice(0, MM_N // 2))
        cast(nc.scalar.copy, 0, 1, slice(MM_N // 2, MM_N))
        cast(nc.vector.tensor_copy, 0, 1, blocks[1])
        for cols in blocks:
            quantize(nc, x_codes[0], x_scales[0], x_grouped[0], cols)
        nc.vector.transpose(out=bias[:], in_=bias_rows[:])
        for cols in blocks:
            multiply(0, 0, cols)
        multiply_skewed(0, range(1, G))

        for r in range(2):
            cast_shared(1, r)
        finish(0, 0)
        for cols in blocks:
            quantize(nc, x_codes[1], x_scales[1], x_grouped[1], cols)
        multiply_skewed(1, range(G))
        for h, g in [(0, g) for g in range(1, G)] + [(1, g) for g in range(G)]:
            finish(h, g)
